import numpy as np
import ml_dtypes


def mxq(x, axis, fmt="e4m3"):
    dtype, down = {"e4m3": (ml_dtypes.float8_e4m3fn, 7), "e5m2": (ml_dtypes.float8_e5m2, 14)}[fmt]
    v = np.moveaxis(np.asarray(x, np.float32).astype(ml_dtypes.bfloat16).astype(np.float64), axis, -1)
    blocks = v.reshape(v.shape[:-1] + (-1, 32))
    amax = np.abs(blocks).max(-1, keepdims=True)
    byte = np.maximum(np.where(amax > 0, np.frexp(amax)[1] - 1 + 127, 0) - down, 1)
    scale = np.exp2(byte - 127.0)
    codes = (blocks / scale).astype(np.float32).astype(dtype).astype(np.float64)
    return np.moveaxis((codes * scale).reshape(v.shape), -1, axis)


WIDE = False


def mx_kscale(k):
    if not WIDE:
        return np.ones(k)
    levels = np.array([10, -10, 5, -5, 0])
    if k % 512:
        return np.exp2(np.random.permutation(np.resize(levels, k // 32))).repeat(32)
    a = np.empty((k // 512, 16))
    for p in range(k // 512):
        a[p, :8] = np.random.permutation(np.resize(levels, 8))
        for g in range(8):
            far = levels[np.abs(levels - a[p, g]) >= 10]
            a[p, g + 8] = far[np.random.randint(len(far))]
    return np.exp2(a.ravel()).repeat(32)


def f64(x):
    return np.asarray(x).astype(np.float64)


def striped(idx):
    return np.tile(np.asarray(idx).reshape(-1, 16).T, (8, 1)).astype(np.uint16)


def unstriped(offs):
    return offs[:16].T.reshape(-1).astype(np.int64)


E2M1 = np.array([0.0, 0.5, 1.0, 1.5, 2.0, 3.0, 4.0, 6.0, -0.0, -0.5, -1.0, -1.5, -2.0, -3.0, -4.0, -6.0])


def pack_weight(w, fmt):
    k, n = w.shape
    w = f64(np.asarray(w, np.float32).astype(ml_dtypes.bfloat16)).reshape(k // 32, 32, n)
    amax = np.abs(w).max(1)
    if fmt == "e4m3":
        byte = np.frexp(amax)[1] - 1 + 127 - 7
    else:
        mant, ex = np.frexp(amax / 6.0)
        byte = np.where(mant > 0.5, ex, ex - 1) + 127
    byte = np.clip(np.where(amax > 0, byte, 1), 1, 254)
    scaled = (w * np.exp2(127.0 - byte)[:, None, :]).reshape(k, n).astype(np.float32)
    by_word = np.ascontiguousarray(scaled.reshape(k // 512, 128, 4, n).transpose(0, 1, 3, 2))
    if fmt == "e4m3":
        words = by_word.astype(ml_dtypes.float8_e4m3fn).view(np.uint8)
    else:
        c = by_word.astype(ml_dtypes.float4_e2m1fn).view(np.uint8) & 0xF
        words = (c[..., 0::2] | (c[..., 1::2] << 4)).reshape(k // 512, 128, 2 * n)
    return np.ascontiguousarray(words), np.ascontiguousarray(byte.astype(np.uint8).reshape(k // 512, 16, n))


def unpack_weight(words, scales, fmt):
    g, _, n = scales.shape
    words = np.ascontiguousarray(words).reshape(g, 128, n, -1)
    if fmt == "e4m3":
        vals = words.view(ml_dtypes.float8_e4m3fn).astype(np.float64)
    else:
        nib = np.empty((g, 128, n, 4), np.uint8)
        nib[..., 0::2] = words & 0xF
        nib[..., 1::2] = words >> 4
        vals = E2M1[nib]
    vals = vals * np.repeat(np.exp2(scales.astype(np.float64) - 127.0), 8, axis=1)[..., None]
    return vals.transpose(0, 1, 3, 2).reshape(g * 512, n)


def sigmoid(v):
    return 1.0 / (1.0 + np.exp(-v))


K, T, J, R, F, Z, O, N, S = 512, 1024, 256, 512, 512, 1024, 128, 256, 1024


def setup_inputs():
    n = np.random.standard_normal
    idx = np.random.permutation(T)[:J]
    idx2 = np.random.permutation(Z)[:J]
    idx3 = np.random.permutation(J)[:O]
    idx4 = np.random.permutation(J)[:O]
    idx5 = np.random.permutation(J)[:O]
    idx6 = np.random.permutation(J)[:O]
    idx7 = np.random.permutation(S)[:N]
    ff = mx_kscale(F)
    fk = mx_kscale(K)
    fr = mx_kscale(R)
    xop = pack_weight(n((F, Z)) / ff[:, None], "e4m3")
    wp = pack_weight(n((K, R)) * 1 / np.sqrt(K) / fk[:, None], "e2m1")
    w2p = pack_weight(n((F, R)) * 1 / np.sqrt(F) * ff[:, None], "e2m1")
    vsp = pack_weight(n((R, S)) * 1 / np.sqrt(R) / fr[:, None], "e2m1")
    return {
        "xo_words": xop[0],
        "xo_scales": xop[1],
        "cq": (np.random.randint(-7, 8, (K, T)).astype(np.float64)).astype(np.float32),
        "gs": (np.random.uniform(0.1, 0.4, (K, 1)) * fk[:, None]).astype(np.float32),
        "w_words": wp[0],
        "w_scales": wp[1],
        "w2_words": w2p[0],
        "w2_scales": w2p[1],
        "sa": (np.random.uniform(0.5, 1.6, (R, 1)) * fr[:, None]).astype(np.float32),
        "sb": (np.random.uniform(0.5, 1.6, (R, 1)) * fr[:, None]).astype(np.float32),
        "bg": (np.random.uniform(-2.0, 2.0, (R, 1))).astype(np.float32),
        "bh": (np.random.uniform(-2.0, 2.0, (R, 1))).astype(np.float32),
        "vs_words": vsp[0],
        "vs_scales": vsp[1],
        "offs": striped(idx),
        "offs2": striped(idx2),
        "offs3": striped(idx3),
        "offs4": striped(idx4),
        "offs5": striped(idx5),
        "offs6": striped(idx6),
        "offs7": striped(idx7),
    }


def reference(xo_words, xo_scales, cq, gs, w_words, w_scales, w2_words, w2_scales, sa, sb, bg, bh, vs_words, vs_scales, offs, offs2, offs3, offs4, offs5, offs6, offs7):
    idx = unstriped(offs)
    idx2 = unstriped(offs2)
    idx3 = unstriped(offs3)
    idx4 = unstriped(offs4)
    idx5 = unstriped(offs5)
    idx6 = unstriped(offs6)
    idx7 = unstriped(offs7)
    xou = unpack_weight(xo_words, xo_scales, "e4m3")
    wu = unpack_weight(w_words, w_scales, "e2m1")
    w2u = unpack_weight(w2_words, w2_scales, "e2m1")
    vsu = unpack_weight(vs_words, vs_scales, "e2m1")
    x1 = f64(cq)[:, idx] * f64(gs)
    x1q = mxq(x1, 0, "e4m3")
    a = wu.T @ x1q
    xoidx2g = xou[:, idx2]
    b = w2u.T @ xoidx2g
    lb = b[:, 0:1]
    la = a[:, 0:1]
    u1 = a[:, idx3] * f64(sa) * sigmoid(a[:, idx4] * lb + f64(bg))
    u2 = b[:, idx5] * f64(sb) * sigmoid(b[:, idx6] * la + f64(bh))
    hid = np.abs(u1 - u2)
    vsidx7g = vsu[:, idx7]
    hidq = mxq(hid, 0, "e4m3")
    y = vsidx7g.T @ hidq
    return y

@@ -1,0 +1,237 @@
+from contextlib import ExitStack
+
+import concourse.mybir as mybir
+
+F32 = mybir.dt.float32
+BF16 = mybir.dt.bfloat16
+I32 = mybir.dt.int32
+U32 = mybir.dt.uint32
+U16 = mybir.dt.uint16
+U8 = mybir.dt.uint8
+FP8X4 = mybir.dt.float8_e4m3fn_x4
+FP4X4 = mybir.dt.float4_e2m1fn_x4
+ACT = mybir.ActivationFunctionType
+ALU = mybir.AluOpType
+
+P = 128
+PACK = 4
+QUADS = 4
+T, J, R, Z, O, N, S = 1024, 256, 512, 1024, 128, 256, 1024
+HALF = J // 2
+
+FLOPS = 2 * 512 * (R * J + R * J + N * O)
+
+
+def tile_list_slopeboth_codednote_store_plain_kernel(
+    tc, xo_words, xo_scales, cq, gs, w_words, w_scales, w2_words, w2_scales, sa, sb, bg, bh,
+    vs_words, vs_scales, offs, offs2, offs3, offs4, offs5, offs6, offs7, out,
+):
+    nc = tc.nc
+    with ExitStack() as ctx:
+        lists = ctx.enter_context(tc.tile_pool(name="lists", bufs=1))
+        keep = ctx.enter_context(tc.tile_pool(name="keep", bufs=1))
+        psum = ctx.enter_context(tc.psum_pool(name="psum", bufs=1))
+
+        def load_list(src, name):
+            tile = lists.tile(list(src.shape), U16, name=name)
+            nc.sync.dma_start(tile[:], src)
+            return tile
+
+        def load_dealt(engine, src, name):
+            tile = keep.tile([P, PACK], F32, name=name)
+            engine.dma_start(tile[:], src.rearrange("(p t) one -> p (t one)", t=PACK))
+            return tile
+
+        def load_words(engine, src, dtype, columns, name):
+            tile = keep.tile([P, columns], dtype, name=name, align_bytes=64)
+            engine.dma_start(tile[:].bitcast(I32), src.bitcast(I32))
+            return tile
+
+        def load_scale_rows(engine, src, name):
+            columns = src.shape[2]
+            staged = keep.tile([PACK, QUADS, columns], U8, name=name + "_staged")
+            engine.dma_start(
+                staged[:].bitcast(I32), src[0].rearrange("(q r) c -> r q c", r=PACK).bitcast(I32)
+            )
+            plane = keep.tile([P, columns], U8, name=name + "_plane", align_bytes=64)
+            nc.vector.memset(plane[:].bitcast(I32), 0)
+            return staged, plane
+
+        def load_cq(t):
+            tile = keep.tile([P, T], F32, name="cq%d" % t)
+            nc.sync.dma_start(tile[:], cq.rearrange("(p t) c -> p t c", t=PACK)[:, t, :])
+            return tile
+
+        list2 = load_list(offs2, "list2")
+        xo_staged, xo_plane = load_scale_rows(nc.scalar, xo_scales, "xo")
+        list1 = load_list(offs, "list1")
+        w2_staged, w2_plane = load_scale_rows(nc.scalar, w2_scales, "w2")
+        xo_raw = load_words(nc.sync, xo_words[0].rearrange("p c r -> p (c r)"), U32, Z, "xo_raw")
+        w2_raw = load_words(nc.scalar, w2_words[0], U16, R, "w2_raw")
+        cq_rows = [load_cq(0)]
+        gs_t = load_dealt(nc.scalar, gs, "gs_t")
+        w_staged, w_plane = load_scale_rows(nc.sync, w_scales, "w")
+        vs_staged, vs_plane = load_scale_rows(nc.sync, vs_scales, "vs")
+        list7 = load_list(offs7, "list7")
+        for t in range(1, PACK):
+            cq_rows.append(load_cq(t))
+        w_raw = load_words(nc.sync, w_words[0], U16, R, "w_raw")
+        list5 = load_list(offs5, "list5")
+        list6 = load_list(offs6, "list6")
+        list3 = load_list(offs3, "list3")
+        list4 = load_list(offs4, "list4")
+        vs_raw = load_words(nc.sync, vs_words[0], U16, S, "vs_raw")
+        sb_t = load_dealt(nc.gpsimd, sb, "sb_t")
+        bh_t = load_dealt(nc.gpsimd, bh, "bh_t")
+        sa_t = load_dealt(nc.gpsimd, sa, "sa_t")
+        bg_t = load_dealt(nc.gpsimd, bg, "bg_t")
+
+        def spread_scale_rows(*pairs):
+            for q in range(QUADS):
+                for staged, plane in pairs:
+                    nc.vector.tensor_copy(
+                        out=plane[32 * q : 32 * q + PACK, :].bitcast(I32), in_=staged[:, q, :].bitcast(I32)
+                    )
+
+        def deal_columns(copy, raw, dtype, run, name, tag=""):
+            dealt = keep.tile([P, PACK, P], dtype, name=name, tag=tag, align_bytes=64)
+            copy(
+                out=dealt[:].rearrange("p t (c i) -> p c t i", i=run),
+                in_=raw[:].rearrange("p (c i t) -> p c t i", i=run, t=PACK),
+            )
+            return dealt
+
+        def gather(window, offsets, dtype, name, tag=""):
+            picked = keep.tile([P, J], dtype, name=name, tag=tag, align_bytes=64)
+            nc.vector.tensor_copy(out=picked[:], in_=window[:].indirect(offsets[:]))
+            return picked
+
+        x1 = keep.tile([P, PACK, J], BF16, name="x1")
+        for t in range(PACK):
+            nc.scalar.activation(
+                out=x1[:, t, :], in_=cq_rows[t][:].indirect(list1[:]), func=ACT.Copy, scale=gs_t[:, t : t + 1]
+            )
+        x1_woven = keep.tile([P, J, PACK], BF16, name="x1_woven", align_bytes=64)
+        x1_codes = keep.tile([P, J], U32, name="x1_codes", align_bytes=64)
+        x1_sc = keep.tile([P, J], U8, name="x1_sc", align_bytes=64)
+        halves = [slice(h * HALF, (h + 1) * HALF) for h in range(2)]
+        last = PACK - 1
+        nc.vector.tensor_copy(out=x1_woven[:, :, :last], in_=x1[:, :last, :].rearrange("p t j -> p j t"))
+        for cols in halves:
+            nc.vector.tensor_copy(out=x1_woven[:, cols, last], in_=x1[:, last, cols])
+        for cols in halves:
+            nc.vector.quantize_mx(
+                out=x1_codes[:, cols].bitcast(FP8X4), scales=x1_sc[:, cols],
+                in_=x1_woven[:, cols, :].rearrange("p j t -> p (j t)"),
+            )
+
+        spread_scale_rows((xo_staged, xo_plane), (w2_staged, w2_plane))
+        w2_codes = deal_columns(nc.scalar.copy, w2_raw, U16, 8, "w2_codes")
+        w2_sc = deal_columns(nc.vector.tensor_copy, w2_plane, U8, 16, "w2_sc")
+        xo_sc = gather(xo_plane, list2, U8, "xo_sc")
+        xo_codes = gather(xo_raw, list2, U32, "xo_codes")
+        b_rows = []
+        for t in range(PACK):
+            acc = psum.tile([P, J], F32, tag="bank%d" % t, name="b_acc%d" % t)
+            nc.tensor.matmul_mx(
+                out=acc[:], lhsT=w2_codes[:, t, :].bitcast(FP4X4), lhsT_scale=w2_sc[:, t, :],
+                rhs=xo_codes[:].bitcast(FP8X4), rhs_scale=xo_sc[:], start=True, stop=True,
+            )
+            rows = keep.tile([P, J], F32, name="b_rows%d" % t)
+            nc.scalar.copy(out=rows[:], in_=acc[:])
+            b_rows.append(rows)
+
+        spread_scale_rows((w_staged, w_plane), (vs_staged, vs_plane))
+        w_sc = deal_columns(nc.vector.tensor_copy, w_plane, U8, 16, "w_sc")
+        w_codes = deal_columns(nc.vector.tensor_copy, w_raw, U16, 8, "w_codes", tag="fp4_stationary")
+        vs_sc = gather(vs_plane, list7, U8, "vs_sc")
+
+        g5 = keep.tile([P, PACK, O], F32, name="g5")
+        for t in range(PACK):
+            nc.scalar.activation(
+                out=g5[:, t, :], in_=b_rows[t][:].indirect(list5[:]), func=ACT.Copy, scale=sb_t[:, t : t + 1]
+            )
+
+        a_rows = [keep.tile([P, J], F32, name="a_rows%d" % t) for t in range(PACK)]
+        s6 = keep.tile([P, PACK, O], F32, name="s6")
+        for h, cols in enumerate(halves):
+            for t in range(PACK):
+                acc = psum.tile([P, HALF], F32, tag="bank%d" % (PACK * (1 - h) + t), name="a_acc%d_%d" % (h, t))
+                nc.tensor.matmul_mx(
+                    out=acc[:], lhsT=w_codes[:, t, :].bitcast(FP4X4), lhsT_scale=w_sc[:, t, :],
+                    rhs=x1_codes[:, cols].bitcast(FP8X4), rhs_scale=x1_sc[:, cols], start=True, stop=True,
+                )
+                nc.vector.tensor_copy(out=a_rows[t][:, cols], in_=acc[:])
+        for t in range(PACK):
+            nc.scalar.activation(
+                out=s6[:, t, :], in_=b_rows[t][:].indirect(list6[:]), func=ACT.Sigmoid,
+                scale=a_rows[t][:, 0:1], bias=bh_t[:, t : t + 1],
+            )
+
+        vs_codes = gather(vs_raw, list7, U16, "vs_codes", tag="fp4_stationary")
+
+        g3 = keep.tile([P, PACK, O], F32, name="g3")
+        s4 = keep.tile([P, PACK, O], F32, name="s4")
+        places = [slice(h * O // 2, (h + 1) * O // 2) for h in range(2)]
+        entries = [slice(h * O // 32, (h + 1) * O // 32) for h in range(2)]
+
+        def gate_a(t, cols, offsets):
+            nc.scalar.activation(
+                out=s4[:, t, cols], in_=a_rows[t][:].indirect(offsets), func=ACT.Sigmoid,
+                scale=b_rows[t][:, 0:1], bias=bg_t[:, t : t + 1],
+            )
+
+        for t in range(PACK):
+            nc.scalar.activation(
+                out=g3[:, t, :], in_=a_rows[t][:].indirect(list3[:]), func=ACT.Copy, scale=sa_t[:, t : t + 1]
+            )
+            if t < last:
+                gate_a(t, slice(0, O), list4[:])
+        for cols, part in zip(places, entries):
+            gate_a(last, cols, list4[:, part])
+
+        u2 = keep.tile([P, PACK, O], F32, name="u2")
+        u1 = keep.tile([P, PACK, O], F32, name="u1")
+        diff = keep.tile([P, PACK, O], F32, name="diff")
+        hid = keep.tile([P, O, PACK], BF16, name="hid", align_bytes=64)
+        hid_codes = keep.tile([P, O], U32, name="hid_codes", align_bytes=64)
+        hid_sc = keep.tile([P, O], U8, name="hid_sc", align_bytes=64)
+        nc.vector.tensor_tensor(out=u2[:], in0=g5[:], in1=s6[:], op=ALU.mult)
+
+        def product(ts, cols):
+            nc.vector.tensor_tensor(out=u1[:, ts, cols], in0=g3[:, ts, cols], in1=s4[:, ts, cols], op=ALU.mult)
+
+        def difference(ts, cols):
+            nc.vector.tensor_tensor(out=diff[:, ts, cols], in0=u1[:, ts, cols], in1=u2[:, ts, cols], op=ALU.subtract)
+
+        def magnitude(ts, cols):
+            d = diff[:, ts, cols].rearrange("p t o -> p o t")
+            nc.vector.scalar_tensor_tensor(out=hid[:, cols, ts], in0=d, scalar=-1.0, in1=d, op0=ALU.mult, op1=ALU.max)
+
+        every = slice(0, O)
+        product(slice(0, 2), every)
+        difference(slice(0, 2), every)
+        magnitude(slice(0, 2), every)
+        product(slice(2, 3), every)
+        difference(slice(2, 3), every)
+        for cols in places:
+            product(slice(3, 4), cols)
+        for cols in places:
+            difference(slice(3, 4), cols)
+        for cols in places:
+            magnitude(slice(2, 4), cols)
+        for cols in places:
+            nc.vector.quantize_mx(
+                out=hid_codes[:, cols].bitcast(FP8X4), scales=hid_sc[:, cols],
+                in_=hid[:, cols, :].rearrange("p o t -> p (o t)"),
+            )
+        for h, (copy, queue) in enumerate(((nc.vector.tensor_copy, nc.sync), (nc.scalar.copy, nc.scalar))):
+            rows = slice(h * P, (h + 1) * P)
+            acc = psum.tile([P, O], F32, tag="bank%d" % (PACK + h), name="y_acc%d" % h)
+            nc.tensor.matmul_mx(
+                out=acc[:], lhsT=vs_codes[:, rows].bitcast(FP4X4), lhsT_scale=vs_sc[:, rows],
+                rhs=hid_codes[:].bitcast(FP8X4), rhs_scale=hid_sc[:], start=True, stop=True,
+            )
+            y = keep.tile([P, O], F32, name="y%d" % h)
+            copy(out=y[:], in_=acc[:])
+            queue.dma_start(out[rows, :], y[:])

@@ -86,6 +86,10 @@ def tile_list_slopeboth_codednote_store_plain_kernel(
         sa_t = load_dealt(nc.gpsimd, sa, "sa_t")
         bg_t = load_dealt(nc.gpsimd, bg, "bg_t")
 
+        warm = keep.tile([P, 2], F32, name="warm")
+        nc.vector.memset(warm[:, 0:1], 0.0)
+        nc.scalar.activation(out=warm[:, 1:2], in_=warm[:, 0:1], func=ACT.Sigmoid)
+
         def spread_scale_rows(*pairs):
             for q in range(QUADS):
                 for staged, plane in pairs:

@@ -30,6 +30,7 @@ def tile_list_slopeboth_codednote_store_plain_kernel(
     with ExitStack() as ctx:
         lists = ctx.enter_context(tc.tile_pool(name="lists", bufs=1))
         keep = ctx.enter_context(tc.tile_pool(name="keep", bufs=1))
+        reuse = ctx.enter_context(tc.tile_pool(name="reuse", bufs=1))
         psum = ctx.enter_context(tc.psum_pool(name="psum", bufs=1))
 
         def load_list(src, name):
@@ -58,7 +59,7 @@ def tile_list_slopeboth_codednote_store_plain_kernel(
             return staged, plane
 
         def load_cq(t):
-            tile = keep.tile([P, T], F32, name="cq%d" % t)
+            tile = reuse.tile([P, T], F32, name="cq%d" % t, offset=4 * T * t)
             nc.sync.dma_start(tile[:], cq.rearrange("(p t) c -> p t c", t=PACK)[:, t, :])
             return tile
 
@@ -71,20 +72,23 @@ def tile_list_slopeboth_codednote_store_plain_kernel(
         cq_rows = [load_cq(0)]
         gs_t = load_dealt(nc.scalar, gs, "gs_t")
         w_staged, w_plane = load_scale_rows(nc.sync, w_scales, "w")
-        vs_staged, vs_plane = load_scale_rows(nc.sync, vs_scales, "vs")
-        list7 = load_list(offs7, "list7")
+        vs_plane = keep.tile([P, S], U8, name="vs_plane", align_bytes=64)
+        nc.gpsimd.memset(vs_plane[:].bitcast(I32), 0)
+        for r in range(PACK):
+            nc.gpsimd.dma_start(vs_plane[r:P:32, :].bitcast(I32), vs_scales[0, r : 4 * QUADS : PACK, :].bitcast(I32))
         for t in range(1, PACK):
             cq_rows.append(load_cq(t))
         w_raw = load_words(nc.sync, w_words[0], U16, R, "w_raw")
         list5 = load_list(offs5, "list5")
+        list7 = load_list(offs7, "list7")
         list6 = load_list(offs6, "list6")
         list3 = load_list(offs3, "list3")
+        sa_t = load_dealt(nc.sync, sa, "sa_t")
         list4 = load_list(offs4, "list4")
+        bg_t = load_dealt(nc.sync, bg, "bg_t")
         vs_raw = load_words(nc.sync, vs_words[0], U16, S, "vs_raw")
         sb_t = load_dealt(nc.gpsimd, sb, "sb_t")
         bh_t = load_dealt(nc.gpsimd, bh, "bh_t")
-        sa_t = load_dealt(nc.gpsimd, sa, "sa_t")
-        bg_t = load_dealt(nc.gpsimd, bg, "bg_t")
 
         warm = keep.tile([P, 2], F32, name="warm")
         nc.vector.memset(warm[:, 0:1], 0.0)
@@ -115,7 +119,7 @@ def tile_list_slopeboth_codednote_store_plain_kernel(
             nc.scalar.activation(
                 out=x1[:, t, :], in_=cq_rows[t][:].indirect(list1[:]), func=ACT.Copy, scale=gs_t[:, t : t + 1]
             )
-        x1_woven = keep.tile([P, J, PACK], BF16, name="x1_woven", align_bytes=64)
+        x1_woven = keep.tile([P, J, PACK], BF16, name="x1_woven", tag="woven", align_bytes=64)
         x1_codes = keep.tile([P, J], U32, name="x1_codes", align_bytes=64)
         x1_sc = keep.tile([P, J], U8, name="x1_sc", align_bytes=64)
         halves = [slice(h * HALF, (h + 1) * HALF) for h in range(2)]
@@ -141,14 +145,13 @@ def tile_list_slopeboth_codednote_store_plain_kernel(
                 out=acc[:], lhsT=w2_codes[:, t, :].bitcast(FP4X4), lhsT_scale=w2_sc[:, t, :],
                 rhs=xo_codes[:].bitcast(FP8X4), rhs_scale=xo_sc[:], start=True, stop=True,
             )
-            rows = keep.tile([P, J], F32, name="b_rows%d" % t)
+            rows = reuse.tile([P, J], F32, name="b_rows%d" % t, offset=4 * (T + t * J))
             nc.scalar.copy(out=rows[:], in_=acc[:])
             b_rows.append(rows)
 
-        spread_scale_rows((w_staged, w_plane), (vs_staged, vs_plane))
+        spread_scale_rows((w_staged, w_plane))
         w_sc = deal_columns(nc.vector.tensor_copy, w_plane, U8, 16, "w_sc")
         w_codes = deal_columns(nc.vector.tensor_copy, w_raw, U16, 8, "w_codes", tag="fp4_stationary")
-        vs_sc = gather(vs_plane, list7, U8, "vs_sc")
 
         g5 = keep.tile([P, PACK, O], F32, name="g5")
         for t in range(PACK):
@@ -165,13 +168,15 @@ def tile_list_slopeboth_codednote_store_plain_kernel(
                     out=acc[:], lhsT=w_codes[:, t, :].bitcast(FP4X4), lhsT_scale=w_sc[:, t, :],
                     rhs=x1_codes[:, cols].bitcast(FP8X4), rhs_scale=x1_sc[:, cols], start=True, stop=True,
                 )
-                nc.vector.tensor_copy(out=a_rows[t][:, cols], in_=acc[:])
+                copy = nc.scalar.copy if (h, t) == (0, 0) else nc.vector.tensor_copy
+                copy(out=a_rows[t][:, cols], in_=acc[:])
         for t in range(PACK):
             nc.scalar.activation(
                 out=s6[:, t, :], in_=b_rows[t][:].indirect(list6[:]), func=ACT.Sigmoid,
                 scale=a_rows[t][:, 0:1], bias=bh_t[:, t : t + 1],
             )
 
+        vs_sc = gather(vs_plane, list7, U8, "vs_sc", tag="woven")
         vs_codes = gather(vs_raw, list7, U16, "vs_codes", tag="fp4_stationary")
 
         g3 = keep.tile([P, PACK, O], F32, name="g3")
@@ -200,7 +205,8 @@ def tile_list_slopeboth_codednote_store_plain_kernel(
         hid = keep.tile([P, O, PACK], BF16, name="hid", align_bytes=64)
         hid_codes = keep.tile([P, O], U32, name="hid_codes", align_bytes=64)
         hid_sc = keep.tile([P, O], U8, name="hid_sc", align_bytes=64)
-        nc.vector.tensor_tensor(out=u2[:], in0=g5[:], in1=s6[:], op=ALU.mult)
+        for ts in (slice(0, 2), slice(2, 4)):
+            nc.gpsimd.tensor_tensor(out=u2[:, ts, :], in0=g5[:, ts, :], in1=s6[:, ts, :], op=ALU.mult)
 
         def product(ts, cols):
             nc.vector.tensor_tensor(out=u1[:, ts, cols], in0=g3[:, ts, cols], in1=s4[:, ts, cols], op=ALU.mult)

from contextlib import ExitStack

import concourse.mybir as mybir

F32 = mybir.dt.float32
BF16 = mybir.dt.bfloat16
I32 = mybir.dt.int32
U32 = mybir.dt.uint32
U16 = mybir.dt.uint16
U8 = mybir.dt.uint8
FP8X4 = mybir.dt.float8_e4m3fn_x4
FP4X4 = mybir.dt.float4_e2m1fn_x4
ACT = mybir.ActivationFunctionType
ALU = mybir.AluOpType

P = 128
PACK = 4
QUADS = 4
T, J, R, Z, O, N, S = 1024, 256, 512, 1024, 128, 256, 1024
HALF = J // 2

FLOPS = 2 * 512 * (R * J + R * J + N * O)


def tile_list_slopeboth_codednote_store_plain_kernel(
    tc, xo_words, xo_scales, cq, gs, w_words, w_scales, w2_words, w2_scales, sa, sb, bg, bh,
    vs_words, vs_scales, offs, offs2, offs3, offs4, offs5, offs6, offs7, out,
):
    nc = tc.nc
    with ExitStack() as ctx:
        lists = ctx.enter_context(tc.tile_pool(name="lists", bufs=1))
        keep = ctx.enter_context(tc.tile_pool(name="keep", bufs=1))
        reuse = ctx.enter_context(tc.tile_pool(name="reuse", bufs=1))
        psum = ctx.enter_context(tc.psum_pool(name="psum", bufs=1))

        def load_list(src, name):
            tile = lists.tile(list(src.shape), U16, name=name)
            nc.sync.dma_start(tile[:], src)
            return tile

        def load_dealt(engine, src, name):
            tile = keep.tile([P, PACK], F32, name=name)
            engine.dma_start(tile[:], src.rearrange("(p t) one -> p (t one)", t=PACK))
            return tile

        def load_words(engine, src, dtype, columns, name):
            tile = keep.tile([P, columns], dtype, name=name, align_bytes=64)
            engine.dma_start(tile[:].bitcast(I32), src.bitcast(I32))
            return tile

        def load_scale_rows(engine, src, name):
            columns = src.shape[2]
            staged = keep.tile([PACK, QUADS, columns], U8, name=name + "_staged")
            engine.dma_start(
                staged[:].bitcast(I32), src[0].rearrange("(q r) c -> r q c", r=PACK).bitcast(I32)
            )
            plane = keep.tile([P, columns], U8, name=name + "_plane", align_bytes=64)
            nc.vector.memset(plane[:].bitcast(I32), 0)
            return staged, plane

        def load_cq(t):
            tile = reuse.tile([P, T], F32, name="cq%d" % t, offset=4 * T * t)
            nc.sync.dma_start(tile[:], cq.rearrange("(p t) c -> p t c", t=PACK)[:, t, :])
            return tile

        list2 = load_list(offs2, "list2")
        xo_staged, xo_plane = load_scale_rows(nc.scalar, xo_scales, "xo")
        list1 = load_list(offs, "list1")
        w2_staged, w2_plane = load_scale_rows(nc.scalar, w2_scales, "w2")
        xo_raw = load_words(nc.sync, xo_words[0].rearrange("p c r -> p (c r)"), U32, Z, "xo_raw")
        w2_raw = load_words(nc.scalar, w2_words[0], U16, R, "w2_raw")
        cq_rows = [load_cq(0)]
        gs_t = load_dealt(nc.scalar, gs, "gs_t")
        w_staged, w_plane = load_scale_rows(nc.sync, w_scales, "w")
        vs_plane = keep.tile([P, S], U8, name="vs_plane", align_bytes=64)
        nc.gpsimd.memset(vs_plane[:].bitcast(I32), 0)
        for r in range(PACK):
            nc.gpsimd.dma_start(vs_plane[r:P:32, :].bitcast(I32), vs_scales[0, r : 4 * QUADS : PACK, :].bitcast(I32))
        for t in range(1, PACK):
            cq_rows.append(load_cq(t))
        w_raw = load_words(nc.sync, w_words[0], U16, R, "w_raw")
        list5 = load_list(offs5, "list5")
        list7 = load_list(offs7, "list7")
        list6 = load_list(offs6, "list6")
        list3 = load_list(offs3, "list3")
        sa_t = load_dealt(nc.sync, sa, "sa_t")
        list4 = load_list(offs4, "list4")
        bg_t = load_dealt(nc.sync, bg, "bg_t")
        vs_raw = load_words(nc.sync, vs_words[0], U16, S, "vs_raw")
        sb_t = load_dealt(nc.gpsimd, sb, "sb_t")
        bh_t = load_dealt(nc.gpsimd, bh, "bh_t")

        warm = keep.tile([P, 2], F32, name="warm")
        nc.vector.memset(warm[:, 0:1], 0.0)
        nc.scalar.activation(out=warm[:, 1:2], in_=warm[:, 0:1], func=ACT.Sigmoid)

        def spread_scale_rows(*pairs):
            for q in range(QUADS):
                for staged, plane in pairs:
                    nc.vector.tensor_copy(
                        out=plane[32 * q : 32 * q + PACK, :].bitcast(I32), in_=staged[:, q, :].bitcast(I32)
                    )

        def deal_columns(copy, raw, dtype, run, name, tag=""):
            dealt = keep.tile([P, PACK, P], dtype, name=name, tag=tag, align_bytes=64)
            copy(
                out=dealt[:].rearrange("p t (c i) -> p c t i", i=run),
                in_=raw[:].rearrange("p (c i t) -> p c t i", i=run, t=PACK),
            )
            return dealt

        def gather(window, offsets, dtype, name, tag=""):
            picked = keep.tile([P, J], dtype, name=name, tag=tag, align_bytes=64)
            nc.vector.tensor_copy(out=picked[:], in_=window[:].indirect(offsets[:]))
            return picked

        x1 = keep.tile([P, PACK, J], BF16, name="x1")
        for t in range(PACK):
            nc.scalar.activation(
                out=x1[:, t, :], in_=cq_rows[t][:].indirect(list1[:]), func=ACT.Copy, scale=gs_t[:, t : t + 1]
            )
        x1_woven = keep.tile([P, J, PACK], BF16, name="x1_woven", tag="woven", align_bytes=64)
        x1_codes = keep.tile([P, J], U32, name="x1_codes", align_bytes=64)
        x1_sc = keep.tile([P, J], U8, name="x1_sc", align_bytes=64)
        halves = [slice(h * HALF, (h + 1) * HALF) for h in range(2)]
        last = PACK - 1
        nc.vector.tensor_copy(out=x1_woven[:, :, :last], in_=x1[:, :last, :].rearrange("p t j -> p j t"))
        for cols in halves:
            nc.vector.tensor_copy(out=x1_woven[:, cols, last], in_=x1[:, last, cols])
        for cols in halves:
            nc.vector.quantize_mx(
                out=x1_codes[:, cols].bitcast(FP8X4), scales=x1_sc[:, cols],
                in_=x1_woven[:, cols, :].rearrange("p j t -> p (j t)"),
            )

        spread_scale_rows((xo_staged, xo_plane), (w2_staged, w2_plane))
        w2_codes = deal_columns(nc.scalar.copy, w2_raw, U16, 8, "w2_codes")
        w2_sc = deal_columns(nc.vector.tensor_copy, w2_plane, U8, 16, "w2_sc")
        xo_sc = gather(xo_plane, list2, U8, "xo_sc")
        xo_codes = gather(xo_raw, list2, U32, "xo_codes")
        b_rows = []
        for t in range(PACK):
            acc = psum.tile([P, J], F32, tag="bank%d" % t, name="b_acc%d" % t)
            nc.tensor.matmul_mx(
                out=acc[:], lhsT=w2_codes[:, t, :].bitcast(FP4X4), lhsT_scale=w2_sc[:, t, :],
                rhs=xo_codes[:].bitcast(FP8X4), rhs_scale=xo_sc[:], start=True, stop=True,
            )
            rows = reuse.tile([P, J], F32, name="b_rows%d" % t, offset=4 * (T + t * J))
            nc.scalar.copy(out=rows[:], in_=acc[:])
            b_rows.append(rows)

        spread_scale_rows((w_staged, w_plane))
        w_sc = deal_columns(nc.vector.tensor_copy, w_plane, U8, 16, "w_sc")
        w_codes = deal_columns(nc.vector.tensor_copy, w_raw, U16, 8, "w_codes", tag="fp4_stationary")

        g5 = keep.tile([P, PACK, O], F32, name="g5")
        for t in range(PACK):
            nc.scalar.activation(
                out=g5[:, t, :], in_=b_rows[t][:].indirect(list5[:]), func=ACT.Copy, scale=sb_t[:, t : t + 1]
            )

        a_rows = [keep.tile([P, J], F32, name="a_rows%d" % t) for t in range(PACK)]
        s6 = keep.tile([P, PACK, O], F32, name="s6")
        for h, cols in enumerate(halves):
            for t in range(PACK):
                acc = psum.tile([P, HALF], F32, tag="bank%d" % (PACK * (1 - h) + t), name="a_acc%d_%d" % (h, t))
                nc.tensor.matmul_mx(
                    out=acc[:], lhsT=w_codes[:, t, :].bitcast(FP4X4), lhsT_scale=w_sc[:, t, :],
                    rhs=x1_codes[:, cols].bitcast(FP8X4), rhs_scale=x1_sc[:, cols], start=True, stop=True,
                )
                copy = nc.scalar.copy if (h, t) == (0, 0) else nc.vector.tensor_copy
                copy(out=a_rows[t][:, cols], in_=acc[:])
        for t in range(PACK):
            nc.scalar.activation(
                out=s6[:, t, :], in_=b_rows[t][:].indirect(list6[:]), func=ACT.Sigmoid,
                scale=a_rows[t][:, 0:1], bias=bh_t[:, t : t + 1],
            )

        vs_sc = gather(vs_plane, list7, U8, "vs_sc", tag="woven")
        vs_codes = gather(vs_raw, list7, U16, "vs_codes", tag="fp4_stationary")

        g3 = keep.tile([P, PACK, O], F32, name="g3")
        s4 = keep.tile([P, PACK, O], F32, name="s4")
        places = [slice(h * O // 2, (h + 1) * O // 2) for h in range(2)]
        entries = [slice(h * O // 32, (h + 1) * O // 32) for h in range(2)]

        def gate_a(t, cols, offsets):
            nc.scalar.activation(
                out=s4[:, t, cols], in_=a_rows[t][:].indirect(offsets), func=ACT.Sigmoid,
                scale=b_rows[t][:, 0:1], bias=bg_t[:, t : t + 1],
            )

        for t in range(PACK):
            nc.scalar.activation(
                out=g3[:, t, :], in_=a_rows[t][:].indirect(list3[:]), func=ACT.Copy, scale=sa_t[:, t : t + 1]
            )
            if t < last:
                gate_a(t, slice(0, O), list4[:])
        for cols, part in zip(places, entries):
            gate_a(last, cols, list4[:, part])

        u2 = keep.tile([P, PACK, O], F32, name="u2")
        u1 = keep.tile([P, PACK, O], F32, name="u1")
        diff = keep.tile([P, PACK, O], F32, name="diff")
        hid = keep.tile([P, O, PACK], BF16, name="hid", align_bytes=64)
        hid_codes = keep.tile([P, O], U32, name="hid_codes", align_bytes=64)
        hid_sc = keep.tile([P, O], U8, name="hid_sc", align_bytes=64)
        for ts in (slice(0, 2), slice(2, 4)):
            nc.gpsimd.tensor_tensor(out=u2[:, ts, :], in0=g5[:, ts, :], in1=s6[:, ts, :], op=ALU.mult)

        def product(ts, cols):
            nc.vector.tensor_tensor(out=u1[:, ts, cols], in0=g3[:, ts, cols], in1=s4[:, ts, cols], op=ALU.mult)

        def difference(ts, cols):
            nc.vector.tensor_tensor(out=diff[:, ts, cols], in0=u1[:, ts, cols], in1=u2[:, ts, cols], op=ALU.subtract)

        def magnitude(ts, cols):
            d = diff[:, ts, cols].rearrange("p t o -> p o t")
            nc.vector.scalar_tensor_tensor(out=hid[:, cols, ts], in0=d, scalar=-1.0, in1=d, op0=ALU.mult, op1=ALU.max)

        every = slice(0, O)
        product(slice(0, 2), every)
        difference(slice(0, 2), every)
        magnitude(slice(0, 2), every)
        product(slice(2, 3), every)
        difference(slice(2, 3), every)
        for cols in places:
            product(slice(3, 4), cols)
        for cols in places:
            difference(slice(3, 4), cols)
        for cols in places:
            magnitude(slice(2, 4), cols)
        for cols in places:
            nc.vector.quantize_mx(
                out=hid_codes[:, cols].bitcast(FP8X4), scales=hid_sc[:, cols],
                in_=hid[:, cols, :].rearrange("p o t -> p (o t)"),
            )
        for h, (copy, queue) in enumerate(((nc.vector.tensor_copy, nc.sync), (nc.scalar.copy, nc.scalar))):
            rows = slice(h * P, (h + 1) * P)
            acc = psum.tile([P, O], F32, tag="bank%d" % (PACK + h), name="y_acc%d" % h)
            nc.tensor.matmul_mx(
                out=acc[:], lhsT=vs_codes[:, rows].bitcast(FP4X4), lhsT_scale=vs_sc[:, rows],
                rhs=hid_codes[:].bitcast(FP8X4), rhs_scale=hid_sc[:], start=True, stop=True,
            )
            y = keep.tile([P, O], F32, name="y%d" % h)
            copy(out=y[:], in_=acc[:])
            queue.dma_start(out[rows, :], y[:])
